import numpy as np
import ml_dtypes


def mxq(x, axis, fmt="e4m3"):
    dtype, down = {"e4m3": (ml_dtypes.float8_e4m3fn, 7), "e5m2": (ml_dtypes.float8_e5m2, 14)}[fmt]
    v = np.moveaxis(np.asarray(x, np.float32).astype(ml_dtypes.bfloat16).astype(np.float64), axis, -1)
    blocks = v.reshape(v.shape[:-1] + (-1, 32))
    amax = np.abs(blocks).max(-1, keepdims=True)
    byte = np.maximum(np.where(amax > 0, np.frexp(amax)[1] - 1 + 127, 0) - down, 1)
    scale = np.exp2(byte - 127.0)
    codes = (blocks / scale).astype(np.float32).astype(dtype).astype(np.float64)
    return np.moveaxis((codes * scale).reshape(v.shape), -1, axis)


WIDE = False


def mx_kscale(k, group=512):
    if not WIDE:
        return np.ones(k)
    levels = np.array([10, -10, 5, -5, 0])
    if group != 512:
        return np.exp2(np.random.permutation(np.resize(levels, k // group))).repeat(group)
    if k % 512:
        return np.exp2(np.random.permutation(np.resize(levels, k // 32))).repeat(32)
    a = np.empty((k // 512, 16))
    for p in range(k // 512):
        a[p, :8] = np.random.permutation(np.resize(levels, 8))
        for g in range(8):
            far = levels[np.abs(levels - a[p, g]) >= 10]
            a[p, g + 8] = far[np.random.randint(len(far))]
    return np.exp2(a.ravel()).repeat(32)


def f64(x):
    return np.asarray(x).astype(np.float64)


G, D, I, N, E, O = 2, 256, 256, 512, 256, 256


def sgn(shape):
    return np.random.uniform(0.5, 2.0, shape) * np.where(np.random.standard_normal(shape) < 0, -1.0, 1.0)


def setup_inputs():
    n = np.random.standard_normal
    s_d = mx_kscale(D, 0)
    s_i = mx_kscale(I, 0)
    s_ge = mx_kscale(G * E).reshape(G, E)
    return {
        "kT": (n((G, D, I)) / np.sqrt(D) / s_d[:, None]).astype(np.float32),
        "qT": (n((G, D, N)) * s_d[:, None]).astype(np.float32),
        "t": (sgn((G, I, 1)) * s_i[:, None]).astype(np.float32),
        "v": (n((G, I, E)) / np.sqrt(I) / s_i[:, None] * s_ge[:, None, :]).astype(np.float32),
        "wo": (n((G, E, O)) / np.sqrt(G * E) / s_ge[:, :, None]).astype(np.float32),
        "r": (n((O, N))).astype(np.float32),
    }


def reference(kT, qT, t, v, wo, r):
    kTq = mxq(f64(kT), 1, "e4m3")
    qTq = mxq(f64(qT), 1, "e4m3")
    z = kTq.transpose(0, 2, 1) @ qTq
    p = np.maximum(z, 0.0) * f64(t)
    vq = mxq(f64(v), 1, "e4m3")
    pq = mxq(p, 1, "e4m3")
    y = vq.transpose(0, 2, 1) @ pq
    woq = mxq((f64(wo)).reshape(G * E, -1), 0, "e4m3")
    yq = mxq((y).reshape(G * E, -1), 0, "e4m3")
    u = woq.T @ yq
    out_ = u + f64(r)
    return out_

@@ -1,0 +1,214 @@
+from contextlib import ExitStack
+
+import concourse.mybir as mybir
+
+G, D, I, N, E, O = 2, 256, 256, 512, 256, 256
+FLOPS = 2 * G * D * I * N + 2 * G * I * E * N + 2 * G * E * O * N
+
+F32 = mybir.dt.float32
+BF16 = mybir.dt.bfloat16
+I32 = mybir.dt.int32
+U8 = mybir.dt.uint8
+FP8X4 = mybir.dt.float8_e4m3fn_x4
+ALU = mybir.AluOpType
+
+P = 128
+R = 64
+PACK = 4
+NC = 128
+UNIT = 2 * NC
+UNITS = N // UNIT
+PADDED = (2 * PACK + 1) * R
+VEC_SHARE = 40
+
+
+def tile_rows_heads_relu_res_kernel(tc, kT, qT, t, v, wo, r, out):
+    nc = tc.nc
+    with ExitStack() as ctx:
+        sb = ctx.enter_context(tc.tile_pool(name="sb", bufs=1))
+        ps = ctx.enter_context(tc.psum_pool(name="ps", bufs=1))
+        ctx.enter_context(tc.manual_schedule())
+
+        def sbuf(name, shape, dtype):
+            return sb.tile(shape, dtype, name=name, align_bytes=64)
+
+        def operand(name, columns):
+            raw = sbuf(name, [P, 5 * columns], U8)
+            return raw, raw[:, 0 : 4 * columns].bitcast(I32), raw[:, 4 * columns : 5 * columns]
+
+        def quantize(words, scales, c0, columns, src):
+            nc.vector.quantize_mx(
+                out=words[:, c0 : c0 + columns].bitcast(FP8X4), scales=scales[:, c0 : c0 + columns], in_=src
+            )
+
+        def mm(dst, rows, lw, ls, l0, rw, rs, r0, start, stop):
+            nc.tensor.matmul_mx(
+                out=dst,
+                lhsT=lw[rows, l0 : l0 + P].bitcast(FP8X4),
+                lhsT_scale=ls[rows, l0 : l0 + P],
+                rhs=rw[rows, r0 : r0 + NC].bitcast(FP8X4),
+                rhs_scale=rs[rows, r0 : r0 + NC],
+                start=start,
+                stop=stop,
+            )
+
+        def copy(on_vector, dst, src):
+            if on_vector:
+                nc.vector.tensor_copy(out=dst, in_=src)
+            else:
+                nc.scalar.copy(out=dst, in_=src)
+
+        def half(h):
+            return slice(R * h, R * (h + 1))
+
+        k_f = sbuf("k_f", [P, PACK, I], F32)
+        v_f = sbuf("v_f", [P, PACK, E], F32)
+        wo_f = sbuf("wo_f", [P, PACK, O], F32)
+        q_f = [sbuf("q_f%d" % u, [P, PACK, UNIT], F32) for u in range(UNITS)]
+        r_f = sbuf("r_f", [P, 2, N], F32)
+        t_f = [sbuf("t_f%d" % g, [P, PACK], F32) for g in range(G)]
+        k_b = sbuf("k_b", [P, PACK * I], BF16)
+        v_b = sbuf("v_b", [P, PACK * E], BF16)
+        wo_b = sbuf("wo_b", [P, PACK * O], BF16)
+        q_b = [sbuf("q_b%d" % u, [P, PACK * UNIT], BF16) for u in range(UNITS)]
+        p_b = [[sbuf("p_b%d%d" % (u, g), [P, PACK * NC], BF16) for g in range(G)] for u in range(UNITS)]
+        y_b = [[sbuf("y_b%d%d" % (u, h), [P, PACK * NC], BF16) for h in range(2)] for u in range(UNITS)]
+        o_f = [sbuf("o_f%d" % u, [P, 2, UNIT], F32) for u in range(UNITS)]
+        k_x = operand("k_x", PADDED)
+        v_x = operand("v_x", PADDED)
+        v_s = operand("v_s", PADDED)
+        wo_x = operand("wo_x", O)
+        q_x = [operand("q_x%d" % u, UNIT) for u in range(UNITS)]
+        p_x = [[operand("p_x%d%d" % (u, g), NC) for g in range(G)] for u in range(UNITS)]
+        y_x = [[operand("y_x%d%d" % (u, h), NC) for h in range(2)] for u in range(UNITS)]
+        tile_bank = [[ps.tile([P, PACK * NC], F32, name="bank%d%d" % (a, b)) for b in range(3)] for a in range(2)]
+        whole_bank = [ps.tile([P, 2, UNIT], F32, name="whole%d" % u) for u in range(UNITS)]
+
+        def load_rows(dst, src):
+            nc.sync.dma_start(out=dst[:], in_=src.rearrange("g (p x) c -> (g p) x c", x=PACK))
+
+        def deal(dst, src, on_vector):
+            m = slice(0, VEC_SHARE) if on_vector else slice(VEC_SHARE, R)
+            copy(
+                on_vector,
+                dst[:].rearrange("p (j m x) -> p m x j", j=PACK, x=PACK)[:, m],
+                src[:].rearrange("p x (m j) -> p m x j", j=PACK)[:, m],
+            )
+
+        def weave(dst, src, m, on_vector):
+            copy(
+                on_vector,
+                dst[:].rearrange("p (m j x) -> p m x j", j=PACK, x=PACK)[:, m],
+                src[:].rearrange("p x (m j) -> p m x j", j=PACK)[:, m],
+            )
+
+        def quantize_padded(dst, src):
+            for j in range(PACK):
+                quantize(dst[1], dst[2], R * (2 * j + 1), R, src[:, PACK * R * j : PACK * R * (j + 1)])
+
+        def window(j, upper):
+            return 2 * R * j + (0 if upper else R)
+
+        def scores(u):
+            for j in range(PACK):
+                for h in range(2):
+                    for g in range(G):
+                        mm(tile_bank[g][u][:, NC * j : NC * (j + 1)], half(g), k_x[1], k_x[2], window(j, h),
+                           q_x[u][1], q_x[u][2], NC * h, h == 0, h == 1)
+
+        def weigh(u, g):
+            nc.vector.scalar_tensor_tensor(
+                out=p_b[u][g][:].rearrange("p (n j) -> p n j", j=PACK),
+                in0=tile_bank[g][u][:].rearrange("p (j n) -> p n j", j=PACK),
+                scalar=0.0,
+                in1=t_f[g][:].unsqueeze(1).to_broadcast([P, NC, PACK]),
+                op0=ALU.max,
+                op1=ALU.mult,
+            )
+
+        def y_bank(u, h):
+            return tile_bank[h][2 if u == 0 else 0]
+
+        def values(u):
+            for j in range(PACK):
+                for step in range(2):
+                    for h in range(2):
+                        g = h if step == 0 else 1 - h
+                        w = v_x if step == 0 else v_s
+                        mm(y_bank(u, h)[:, NC * j : NC * (j + 1)], half(h), w[1], w[2], window(j, g),
+                           p_x[u][g][1], p_x[u][g][2], 0, step == 0, step == 1)
+
+        def round_y(u, h, on_vector):
+            copy(
+                on_vector,
+                y_b[u][h][:].rearrange("p (n j) -> p n j", j=PACK),
+                y_bank(u, h)[:].rearrange("p (j n) -> p n j", j=PACK),
+            )
+
+        def project(u, h):
+            for c in range(2):
+                mm(whole_bank[u][:, c, NC * h : NC * (h + 1)], slice(0, P), wo_x[1], wo_x[2], P * c,
+                   y_x[u][h][1], y_x[u][h][2], 0, True, True)
+
+        out_v = out.rearrange("(c p) n -> p c n", p=P)
+
+        def finish(u):
+            cols = slice(UNIT * u, UNIT * (u + 1))
+            nc.vector.tensor_tensor(out=o_f[u][:], in0=whole_bank[u][:], in1=r_f[:, :, cols], op=ALU.add)
+            nc.sync.dma_start(out=out_v[:, :, cols], in_=o_f[u][:])
+
+        first = slice(0, VEC_SHARE)
+        rest = slice(VEC_SHARE, R)
+
+        load_rows(k_f, kT)
+        load_rows(q_f[0], qT[:, :, 0:UNIT])
+        load_rows(v_f, v)
+        load_rows(q_f[1], qT[:, :, UNIT:N])
+        for g in range(G):
+            for h in range(2):
+                nc.gpsimd.dma_start(out=t_f[g][half(h), :], in_=t[g].rearrange("(p x) o -> p (x o)", x=PACK))
+        nc.vector.memset(k_x[0][:].bitcast(I32), 0)
+        nc.vector.memset(v_x[0][:].bitcast(I32), 0)
+
+        deal(k_b, k_f, True)
+        deal(k_b, k_f, False)
+        quantize_padded(k_x, k_b)
+        weave(q_b[0], q_f[0], first, True)
+        weave(q_b[0], q_f[0], rest, False)
+        quantize(q_x[0][1], q_x[0][2], 0, UNIT, q_b[0][:])
+        scores(0)
+        deal(v_b, v_f, True)
+        deal(v_b, v_f, False)
+        quantize_padded(v_x, v_b)
+        for h in range(2):
+            nc.sync.dma_start(out=v_s[0][:].bitcast(I32)[half(h), :], in_=v_x[0][:].bitcast(I32)[half(1 - h), :])
+        load_rows(wo_f, wo)
+        nc.sync.dma_start(out=r_f[:], in_=r.rearrange("(c p) n -> p c n", p=P))
+        weave(q_b[1], q_f[1], first, True)
+        weave(q_b[1], q_f[1], rest, False)
+        weigh(0, 0)
+        quantize(q_x[1][1], q_x[1][2], 0, UNIT, q_b[1][:])
+        scores(1)
+        weigh(0, 1)
+        for g in range(G):
+            quantize(p_x[0][g][1], p_x[0][g][2], 0, NC, p_b[0][g][:])
+        values(0)
+        weave(wo_b, wo_f, slice(0, R), False)
+        for g in range(G):
+            weigh(1, g)
+        for g in range(G):
+            quantize(p_x[1][g][1], p_x[1][g][2], 0, NC, p_b[1][g][:])
+        quantize(wo_x[1], wo_x[2], 0, O, wo_b[:])
+        round_y(0, 0, False)
+        round_y(0, 1, False)
+        values(1)
+        for h in range(2):
+            quantize(y_x[0][h][1], y_x[0][h][2], 0, NC, y_b[0][h][:])
+            project(0, h)
+        round_y(1, 0, False)
+        round_y(1, 1, True)
+        finish(0)
+        for h in range(2):
+            quantize(y_x[1][h][1], y_x[1][h][2], 0, NC, y_b[1][h][:])
+            project(1, h)
+        finish(1)

@@ -20,6 +20,10 @@ UNIT = 2 * NC
 UNITS = N // UNIT
 PADDED = (2 * PACK + 1) * R
 VEC_SHARE = 40
+WARM_A = 32
+WARM_B = 8
+WARM_C = 8
+Q1_SHARE = 32
 
 
 def tile_rows_heads_relu_res_kernel(tc, kT, qT, t, v, wo, r, out):
@@ -66,14 +70,16 @@ def tile_rows_heads_relu_res_kernel(tc, kT, qT, t, v, wo, r, out):
         wo_f = sbuf("wo_f", [P, PACK, O], F32)
         q_f = [sbuf("q_f%d" % u, [P, PACK, UNIT], F32) for u in range(UNITS)]
         r_f = sbuf("r_f", [P, 2, N], F32)
-        t_f = [sbuf("t_f%d" % g, [P, PACK], F32) for g in range(G)]
+        t_f = sbuf("t_f", [P, G, 2 * PACK], F32)
+        one_b = sbuf("one_b", [P, PACK * NC], BF16)
+        one_x = operand("one_x", NC)
         k_b = sbuf("k_b", [P, PACK * I], BF16)
         v_b = sbuf("v_b", [P, PACK * E], BF16)
         wo_b = sbuf("wo_b", [P, PACK * O], BF16)
         q_b = [sbuf("q_b%d" % u, [P, PACK * UNIT], BF16) for u in range(UNITS)]
         p_b = [[sbuf("p_b%d%d" % (u, g), [P, PACK * NC], BF16) for g in range(G)] for u in range(UNITS)]
         y_b = [[sbuf("y_b%d%d" % (u, h), [P, PACK * NC], BF16) for h in range(2)] for u in range(UNITS)]
-        o_f = [sbuf("o_f%d" % u, [P, 2, UNIT], F32) for u in range(UNITS)]
+        o_f = [[sbuf("o_f%d%d" % (u, h), [P, 2, NC], F32) for h in range(2)] for u in range(UNITS)]
         k_x = operand("k_x", PADDED)
         v_x = operand("v_x", PADDED)
         v_s = operand("v_s", PADDED)
@@ -82,7 +88,7 @@ def tile_rows_heads_relu_res_kernel(tc, kT, qT, t, v, wo, r, out):
         p_x = [[operand("p_x%d%d" % (u, g), NC) for g in range(G)] for u in range(UNITS)]
         y_x = [[operand("y_x%d%d" % (u, h), NC) for h in range(2)] for u in range(UNITS)]
         tile_bank = [[ps.tile([P, PACK * NC], F32, name="bank%d%d" % (a, b)) for b in range(3)] for a in range(2)]
-        whole_bank = [ps.tile([P, 2, UNIT], F32, name="whole%d" % u) for u in range(UNITS)]
+        whole_bank = [ps.tile([P, 2, NC], F32, name="whole%d" % h) for h in range(2)]
 
         def load_rows(dst, src):
             nc.sync.dma_start(out=dst[:], in_=src.rearrange("g (p x) c -> (g p) x c", x=PACK))
@@ -110,9 +116,9 @@ def tile_rows_heads_relu_res_kernel(tc, kT, qT, t, v, wo, r, out):
             return 2 * R * j + (0 if upper else R)
 
         def scores(u):
-            for j in range(PACK):
-                for h in range(2):
-                    for g in range(G):
+            for g in range(G):
+                for j in range(PACK):
+                    for h in range(2):
                         mm(tile_bank[g][u][:, NC * j : NC * (j + 1)], half(g), k_x[1], k_x[2], window(j, h),
                            q_x[u][1], q_x[u][2], NC * h, h == 0, h == 1)
 
@@ -121,7 +127,7 @@ def tile_rows_heads_relu_res_kernel(tc, kT, qT, t, v, wo, r, out):
                 out=p_b[u][g][:].rearrange("p (n j) -> p n j", j=PACK),
                 in0=tile_bank[g][u][:].rearrange("p (j n) -> p n j", j=PACK),
                 scalar=0.0,
-                in1=t_f[g][:].unsqueeze(1).to_broadcast([P, NC, PACK]),
+                in1=t_f[:, g, 0:PACK].unsqueeze(1).to_broadcast([P, NC, PACK]),
                 op0=ALU.max,
                 op1=ALU.mult,
             )
@@ -129,14 +135,12 @@ def tile_rows_heads_relu_res_kernel(tc, kT, qT, t, v, wo, r, out):
         def y_bank(u, h):
             return tile_bank[h][2 if u == 0 else 0]
 
-        def values(u):
+        def values(u, h):
             for j in range(PACK):
-                for step in range(2):
-                    for h in range(2):
-                        g = h if step == 0 else 1 - h
-                        w = v_x if step == 0 else v_s
-                        mm(y_bank(u, h)[:, NC * j : NC * (j + 1)], half(h), w[1], w[2], window(j, g),
-                           p_x[u][g][1], p_x[u][g][2], 0, step == 0, step == 1)
+                for g in range(G):
+                    w = v_x if g == h else v_s
+                    mm(y_bank(u, h)[:, NC * j : NC * (j + 1)], half(h), w[1], w[2], window(j, g),
+                       p_x[u][g][1], p_x[u][g][2], 0, g == 0, g == 1)
 
         def round_y(u, h, on_vector):
             copy(
@@ -147,15 +151,25 @@ def tile_rows_heads_relu_res_kernel(tc, kT, qT, t, v, wo, r, out):
 
         def project(u, h):
             for c in range(2):
-                mm(whole_bank[u][:, c, NC * h : NC * (h + 1)], slice(0, P), wo_x[1], wo_x[2], P * c,
+                mm(whole_bank[h][:, c, :], slice(0, P), wo_x[1], wo_x[2], P * c,
                    y_x[u][h][1], y_x[u][h][2], 0, True, True)
+
+        def warm(w, c0, count):
+            for i in range(count):
+                mm(whole_bank[1][:, 0, 0:NC], slice(0, P), w[1], w[2], c0, w[1], w[2], c0, True, True)
 
         out_v = out.rearrange("(c p) n -> p c n", p=P)
 
-        def finish(u):
-            cols = slice(UNIT * u, UNIT * (u + 1))
-            nc.vector.tensor_tensor(out=o_f[u][:], in0=whole_bank[u][:], in1=r_f[:, :, cols], op=ALU.add)
-            nc.sync.dma_start(out=out_v[:, :, cols], in_=o_f[u][:])
+        def finish(u, h):
+            cols = slice(UNIT * u + NC * h, UNIT * u + NC * (h + 1))
+            nc.vector.tensor_tensor(out=o_f[u][h][:], in0=whole_bank[h][:], in1=r_f[:, :, cols], op=ALU.add)
+            nc.sync.dma_start(out=out_v[:, :, cols], in_=o_f[u][h][:])
+
+        def quantize_p(u, g):
+            quantize(p_x[u][g][1], p_x[u][g][2], 0, NC, p_b[u][g][:])
+
+        def quantize_y(u, h):
+            quantize(y_x[u][h][1], y_x[u][h][2], 0, NC, y_b[u][h][:])
 
         first = slice(0, VEC_SHARE)
         rest = slice(VEC_SHARE, R)
@@ -164,51 +178,61 @@ def tile_rows_heads_relu_res_kernel(tc, kT, qT, t, v, wo, r, out):
         load_rows(q_f[0], qT[:, :, 0:UNIT])
         load_rows(v_f, v)
         load_rows(q_f[1], qT[:, :, UNIT:N])
-        for g in range(G):
-            for h in range(2):
-                nc.gpsimd.dma_start(out=t_f[g][half(h), :], in_=t[g].rearrange("(p x) o -> p (x o)", x=PACK))
+        load_rows(wo_f, wo)
+        for h in range(2):
+            nc.scalar.dma_start(out=t_f[half(h), :, 0:PACK], in_=t.rearrange("g (p x) o -> p g (x o)", x=PACK))
+        nc.vector.memset(one_b[:], 1.0)
         nc.vector.memset(k_x[0][:].bitcast(I32), 0)
+        quantize(one_x[1], one_x[2], 0, NC, one_b[:])
         nc.vector.memset(v_x[0][:].bitcast(I32), 0)
+        warm(one_x, 0, WARM_A)
 
         deal(k_b, k_f, True)
         deal(k_b, k_f, False)
         quantize_padded(k_x, k_b)
+        warm(k_x, R, WARM_B)
         weave(q_b[0], q_f[0], first, True)
         weave(q_b[0], q_f[0], rest, False)
         quantize(q_x[0][1], q_x[0][2], 0, UNIT, q_b[0][:])
         scores(0)
+        warm(one_x, 0, WARM_C)
         deal(v_b, v_f, True)
         deal(v_b, v_f, False)
         quantize_padded(v_x, v_b)
         for h in range(2):
             nc.sync.dma_start(out=v_s[0][:].bitcast(I32)[half(h), :], in_=v_x[0][:].bitcast(I32)[half(1 - h), :])
-        load_rows(wo_f, wo)
         nc.sync.dma_start(out=r_f[:], in_=r.rearrange("(c p) n -> p c n", p=P))
-        weave(q_b[1], q_f[1], first, True)
-        weave(q_b[1], q_f[1], rest, False)
+        weave(q_b[1], q_f[1], slice(0, Q1_SHARE), True)
+        weave(q_b[1], q_f[1], slice(Q1_SHARE, R), False)
         weigh(0, 0)
         quantize(q_x[1][1], q_x[1][2], 0, UNIT, q_b[1][:])
         scores(1)
         weigh(0, 1)
-        for g in range(G):
-            quantize(p_x[0][g][1], p_x[0][g][2], 0, NC, p_b[0][g][:])
-        values(0)
         weave(wo_b, wo_f, slice(0, R), False)
-        for g in range(G):
-            weigh(1, g)
-        for g in range(G):
-            quantize(p_x[1][g][1], p_x[1][g][2], 0, NC, p_b[1][g][:])
+        quantize_p(0, 0)
+        quantize_p(0, 1)
+        values(0, 0)
+        values(0, 1)
+        weigh(1, 0)
+        weigh(1, 1)
+        quantize_p(1, 0)
+        quantize_p(1, 1)
         quantize(wo_x[1], wo_x[2], 0, O, wo_b[:])
         round_y(0, 0, False)
         round_y(0, 1, False)
-        values(1)
-        for h in range(2):
-            quantize(y_x[0][h][1], y_x[0][h][2], 0, NC, y_b[0][h][:])
-            project(0, h)
+        values(1, 0)
+        quantize_y(0, 0)
+        project(0, 0)
+        values(1, 1)
+        quantize_y(0, 1)
+        project(0, 1)
         round_y(1, 0, False)
-        round_y(1, 1, True)
-        finish(0)
-        for h in range(2):
-            quantize(y_x[1][h][1], y_x[1][h][2], 0, NC, y_b[1][h][:])
-            project(1, h)
-        finish(1)
+        round_y(1, 1, False)
+        finish(0, 0)
+        quantize_y(1, 0)
+        project(1, 0)
+        finish(0, 1)
+        quantize_y(1, 1)
+        project(1, 1)
+        finish(1, 0)
+        finish(1, 1)

@@ -19,7 +19,7 @@ NC = 128
 UNIT = 2 * NC
 UNITS = N // UNIT
 PADDED = (2 * PACK + 1) * R
-VEC_SHARE = 40
+VEC_SHARE = 42
 WARM_A = 32
 WARM_B = 8
 WARM_C = 8
@@ -97,15 +97,15 @@ def tile_rows_heads_relu_res_kernel(tc, kT, qT, t, v, wo, r, out):
             m = slice(0, VEC_SHARE) if on_vector else slice(VEC_SHARE, R)
             copy(
                 on_vector,
-                dst[:].rearrange("p (j m x) -> p m x j", j=PACK, x=PACK)[:, m],
-                src[:].rearrange("p x (m j) -> p m x j", j=PACK)[:, m],
+                dst[:].rearrange("p (j m x) -> p m j x", j=PACK, x=PACK)[:, m],
+                src[:].rearrange("p x (m j) -> p m j x", j=PACK)[:, m],
             )
 
         def weave(dst, src, m, on_vector):
             copy(
                 on_vector,
-                dst[:].rearrange("p (m j x) -> p m x j", j=PACK, x=PACK)[:, m],
-                src[:].rearrange("p x (m j) -> p m x j", j=PACK)[:, m],
+                dst[:].rearrange("p (m j x) -> p m j x", j=PACK, x=PACK)[:, m],
+                src[:].rearrange("p x (m j) -> p m j x", j=PACK)[:, m],
             )
 
         def quantize_padded(dst, src):
@@ -178,9 +178,9 @@ def tile_rows_heads_relu_res_kernel(tc, kT, qT, t, v, wo, r, out):
         load_rows(q_f[0], qT[:, :, 0:UNIT])
         load_rows(v_f, v)
         load_rows(q_f[1], qT[:, :, UNIT:N])
-        load_rows(wo_f, wo)
         for h in range(2):
-            nc.scalar.dma_start(out=t_f[half(h), :, 0:PACK], in_=t.rearrange("g (p x) o -> p g (x o)", x=PACK))
+            nc.sync.dma_start(out=t_f[half(h), :, 0:PACK], in_=t.rearrange("g (p x) o -> p g (x o)", x=PACK))
+        load_rows(wo_f, wo)
         nc.vector.memset(one_b[:], 1.0)
         nc.vector.memset(k_x[0][:].bitcast(I32), 0)
         quantize(one_x[1], one_x[2], 0, NC, one_b[:])

@@ -20,10 +20,10 @@ UNIT = 2 * NC
 UNITS = N // UNIT
 PADDED = (2 * PACK + 1) * R
 VEC_SHARE = 42
-WARM_A = 32
+WARM_A = 28
 WARM_B = 8
-WARM_C = 8
-Q1_SHARE = 32
+WARM_C = 12
+FILL = (2, 4, 2)
 
 
 def tile_rows_heads_relu_res_kernel(tc, kT, qT, t, v, wo, r, out):
@@ -158,6 +158,11 @@ def tile_rows_heads_relu_res_kernel(tc, kT, qT, t, v, wo, r, out):
             for i in range(count):
                 mm(whole_bank[1][:, 0, 0:NC], slice(0, P), w[1], w[2], c0, w[1], w[2], c0, True, True)
 
+        def fill(bank, count):
+            for i in range(count):
+                a = i % 2
+                mm(tile_bank[a][bank][:, 0:NC], half(a), k_x[1], k_x[2], R, q_x[0][1], q_x[0][2], 0, True, True)
+
         out_v = out.rearrange("(c p) n -> p c n", p=P)
 
         def finish(u, h):
@@ -175,8 +180,8 @@ def tile_rows_heads_relu_res_kernel(tc, kT, qT, t, v, wo, r, out):
         rest = slice(VEC_SHARE, R)
 
         load_rows(k_f, kT)
-        load_rows(q_f[0], qT[:, :, 0:UNIT])
         load_rows(v_f, v)
+        load_rows(q_f[0], qT[:, :, 0:UNIT])
         load_rows(q_f[1], qT[:, :, UNIT:N])
         for h in range(2):
             nc.sync.dma_start(out=t_f[half(h), :, 0:PACK], in_=t.rearrange("g (p x) o -> p g (x o)", x=PACK))
@@ -191,45 +196,48 @@ def tile_rows_heads_relu_res_kernel(tc, kT, qT, t, v, wo, r, out):
         deal(k_b, k_f, False)
         quantize_padded(k_x, k_b)
         warm(k_x, R, WARM_B)
+        deal(v_b, v_f, True)
+        deal(v_b, v_f, False)
+        quantize_padded(v_x, v_b)
+        warm(v_x, 2 * R * (PACK - 1), WARM_C)
+        for h in range(2):
+            nc.sync.dma_start(out=v_s[0][:].bitcast(I32)[half(h), :], in_=v_x[0][:].bitcast(I32)[half(1 - h), :])
+        nc.sync.dma_start(out=r_f[:], in_=r.rearrange("(c p) n -> p c n", p=P))
         weave(q_b[0], q_f[0], first, True)
         weave(q_b[0], q_f[0], rest, False)
         quantize(q_x[0][1], q_x[0][2], 0, UNIT, q_b[0][:])
         scores(0)
-        warm(one_x, 0, WARM_C)
-        deal(v_b, v_f, True)
-        deal(v_b, v_f, False)
-        quantize_padded(v_x, v_b)
-        for h in range(2):
-            nc.sync.dma_start(out=v_s[0][:].bitcast(I32)[half(h), :], in_=v_x[0][:].bitcast(I32)[half(1 - h), :])
-        nc.sync.dma_start(out=r_f[:], in_=r.rearrange("(c p) n -> p c n", p=P))
-        weave(q_b[1], q_f[1], slice(0, Q1_SHARE), True)
-        weave(q_b[1], q_f[1], slice(Q1_SHARE, R), False)
-        weigh(0, 0)
+        fill(2, FILL[0])
+        weave(q_b[1], q_f[1], first, True)
+        weave(q_b[1], q_f[1], rest, False)
         quantize(q_x[1][1], q_x[1][2], 0, UNIT, q_b[1][:])
         scores(1)
+        fill(2, FILL[1])
+        weigh(0, 0)
         weigh(0, 1)
         weave(wo_b, wo_f, slice(0, R), False)
         quantize_p(0, 0)
         quantize_p(0, 1)
         values(0, 0)
         values(0, 1)
+        fill(0, FILL[2])
         weigh(1, 0)
         weigh(1, 1)
         quantize_p(1, 0)
         quantize_p(1, 1)
+        values(1, 0)
+        values(1, 1)
         quantize(wo_x[1], wo_x[2], 0, O, wo_b[:])
         round_y(0, 0, False)
         round_y(0, 1, False)
-        values(1, 0)
         quantize_y(0, 0)
         project(0, 0)
-        values(1, 1)
         quantize_y(0, 1)
         project(0, 1)
         round_y(1, 0, False)
         round_y(1, 1, False)
-        finish(0, 0)
         quantize_y(1, 0)
+        finish(0, 0)
         project(1, 0)
         finish(0, 1)
         quantize_y(1, 1)

from contextlib import ExitStack

import concourse.mybir as mybir

G, D, I, N, E, O = 2, 256, 256, 512, 256, 256
FLOPS = 2 * G * D * I * N + 2 * G * I * E * N + 2 * G * E * O * N

F32 = mybir.dt.float32
BF16 = mybir.dt.bfloat16
I32 = mybir.dt.int32
U8 = mybir.dt.uint8
FP8X4 = mybir.dt.float8_e4m3fn_x4
ALU = mybir.AluOpType

P = 128
R = 64
PACK = 4
NC = 128
UNIT = 2 * NC
UNITS = N // UNIT
PADDED = (2 * PACK + 1) * R
VEC_SHARE = 42
WARM_A = 28
WARM_B = 8
WARM_C = 12
FILL = (2, 4, 2)


def tile_rows_heads_relu_res_kernel(tc, kT, qT, t, v, wo, r, out):
    nc = tc.nc
    with ExitStack() as ctx:
        sb = ctx.enter_context(tc.tile_pool(name="sb", bufs=1))
        ps = ctx.enter_context(tc.psum_pool(name="ps", bufs=1))
        ctx.enter_context(tc.manual_schedule())

        def sbuf(name, shape, dtype):
            return sb.tile(shape, dtype, name=name, align_bytes=64)

        def operand(name, columns):
            raw = sbuf(name, [P, 5 * columns], U8)
            return raw, raw[:, 0 : 4 * columns].bitcast(I32), raw[:, 4 * columns : 5 * columns]

        def quantize(words, scales, c0, columns, src):
            nc.vector.quantize_mx(
                out=words[:, c0 : c0 + columns].bitcast(FP8X4), scales=scales[:, c0 : c0 + columns], in_=src
            )

        def mm(dst, rows, lw, ls, l0, rw, rs, r0, start, stop):
            nc.tensor.matmul_mx(
                out=dst,
                lhsT=lw[rows, l0 : l0 + P].bitcast(FP8X4),
                lhsT_scale=ls[rows, l0 : l0 + P],
                rhs=rw[rows, r0 : r0 + NC].bitcast(FP8X4),
                rhs_scale=rs[rows, r0 : r0 + NC],
                start=start,
                stop=stop,
            )

        def copy(on_vector, dst, src):
            if on_vector:
                nc.vector.tensor_copy(out=dst, in_=src)
            else:
                nc.scalar.copy(out=dst, in_=src)

        def half(h):
            return slice(R * h, R * (h + 1))

        k_f = sbuf("k_f", [P, PACK, I], F32)
        v_f = sbuf("v_f", [P, PACK, E], F32)
        wo_f = sbuf("wo_f", [P, PACK, O], F32)
        q_f = [sbuf("q_f%d" % u, [P, PACK, UNIT], F32) for u in range(UNITS)]
        r_f = sbuf("r_f", [P, 2, N], F32)
        t_f = sbuf("t_f", [P, G, 2 * PACK], F32)
        one_b = sbuf("one_b", [P, PACK * NC], BF16)
        one_x = operand("one_x", NC)
        k_b = sbuf("k_b", [P, PACK * I], BF16)
        v_b = sbuf("v_b", [P, PACK * E], BF16)
        wo_b = sbuf("wo_b", [P, PACK * O], BF16)
        q_b = [sbuf("q_b%d" % u, [P, PACK * UNIT], BF16) for u in range(UNITS)]
        p_b = [[sbuf("p_b%d%d" % (u, g), [P, PACK * NC], BF16) for g in range(G)] for u in range(UNITS)]
        y_b = [[sbuf("y_b%d%d" % (u, h), [P, PACK * NC], BF16) for h in range(2)] for u in range(UNITS)]
        o_f = [[sbuf("o_f%d%d" % (u, h), [P, 2, NC], F32) for h in range(2)] for u in range(UNITS)]
        k_x = operand("k_x", PADDED)
        v_x = operand("v_x", PADDED)
        v_s = operand("v_s", PADDED)
        wo_x = operand("wo_x", O)
        q_x = [operand("q_x%d" % u, UNIT) for u in range(UNITS)]
        p_x = [[operand("p_x%d%d" % (u, g), NC) for g in range(G)] for u in range(UNITS)]
        y_x = [[operand("y_x%d%d" % (u, h), NC) for h in range(2)] for u in range(UNITS)]
        tile_bank = [[ps.tile([P, PACK * NC], F32, name="bank%d%d" % (a, b)) for b in range(3)] for a in range(2)]
        whole_bank = [ps.tile([P, 2, NC], F32, name="whole%d" % h) for h in range(2)]

        def load_rows(dst, src):
            nc.sync.dma_start(out=dst[:], in_=src.rearrange("g (p x) c -> (g p) x c", x=PACK))

        def deal(dst, src, on_vector):
            m = slice(0, VEC_SHARE) if on_vector else slice(VEC_SHARE, R)
            copy(
                on_vector,
                dst[:].rearrange("p (j m x) -> p m j x", j=PACK, x=PACK)[:, m],
                src[:].rearrange("p x (m j) -> p m j x", j=PACK)[:, m],
            )

        def weave(dst, src, m, on_vector):
            copy(
                on_vector,
                dst[:].rearrange("p (m j x) -> p m j x", j=PACK, x=PACK)[:, m],
                src[:].rearrange("p x (m j) -> p m j x", j=PACK)[:, m],
            )

        def quantize_padded(dst, src):
            for j in range(PACK):
                quantize(dst[1], dst[2], R * (2 * j + 1), R, src[:, PACK * R * j : PACK * R * (j + 1)])

        def window(j, upper):
            return 2 * R * j + (0 if upper else R)

        def scores(u):
            for g in range(G):
                for j in range(PACK):
                    for h in range(2):
                        mm(tile_bank[g][u][:, NC * j : NC * (j + 1)], half(g), k_x[1], k_x[2], window(j, h),
                           q_x[u][1], q_x[u][2], NC * h, h == 0, h == 1)

        def weigh(u, g):
            nc.vector.scalar_tensor_tensor(
                out=p_b[u][g][:].rearrange("p (n j) -> p n j", j=PACK),
                in0=tile_bank[g][u][:].rearrange("p (j n) -> p n j", j=PACK),
                scalar=0.0,
                in1=t_f[:, g, 0:PACK].unsqueeze(1).to_broadcast([P, NC, PACK]),
                op0=ALU.max,
                op1=ALU.mult,
            )

        def y_bank(u, h):
            return tile_bank[h][2 if u == 0 else 0]

        def values(u, h):
            for j in range(PACK):
                for g in range(G):
                    w = v_x if g == h else v_s
                    mm(y_bank(u, h)[:, NC * j : NC * (j + 1)], half(h), w[1], w[2], window(j, g),
                       p_x[u][g][1], p_x[u][g][2], 0, g == 0, g == 1)

        def round_y(u, h, on_vector):
            copy(
                on_vector,
                y_b[u][h][:].rearrange("p (n j) -> p n j", j=PACK),
                y_bank(u, h)[:].rearrange("p (j n) -> p n j", j=PACK),
            )

        def project(u, h):
            for c in range(2):
                mm(whole_bank[h][:, c, :], slice(0, P), wo_x[1], wo_x[2], P * c,
                   y_x[u][h][1], y_x[u][h][2], 0, True, True)

        def warm(w, c0, count):
            for i in range(count):
                mm(whole_bank[1][:, 0, 0:NC], slice(0, P), w[1], w[2], c0, w[1], w[2], c0, True, True)

        def fill(bank, count):
            for i in range(count):
                a = i % 2
                mm(tile_bank[a][bank][:, 0:NC], half(a), k_x[1], k_x[2], R, q_x[0][1], q_x[0][2], 0, True, True)

        out_v = out.rearrange("(c p) n -> p c n", p=P)

        def finish(u, h):
            cols = slice(UNIT * u + NC * h, UNIT * u + NC * (h + 1))
            nc.vector.tensor_tensor(out=o_f[u][h][:], in0=whole_bank[h][:], in1=r_f[:, :, cols], op=ALU.add)
            nc.sync.dma_start(out=out_v[:, :, cols], in_=o_f[u][h][:])

        def quantize_p(u, g):
            quantize(p_x[u][g][1], p_x[u][g][2], 0, NC, p_b[u][g][:])

        def quantize_y(u, h):
            quantize(y_x[u][h][1], y_x[u][h][2], 0, NC, y_b[u][h][:])

        first = slice(0, VEC_SHARE)
        rest = slice(VEC_SHARE, R)

        load_rows(k_f, kT)
        load_rows(v_f, v)
        load_rows(q_f[0], qT[:, :, 0:UNIT])
        load_rows(q_f[1], qT[:, :, UNIT:N])
        for h in range(2):
            nc.sync.dma_start(out=t_f[half(h), :, 0:PACK], in_=t.rearrange("g (p x) o -> p g (x o)", x=PACK))
        load_rows(wo_f, wo)
        nc.vector.memset(one_b[:], 1.0)
        nc.vector.memset(k_x[0][:].bitcast(I32), 0)
        quantize(one_x[1], one_x[2], 0, NC, one_b[:])
        nc.vector.memset(v_x[0][:].bitcast(I32), 0)
        warm(one_x, 0, WARM_A)

        deal(k_b, k_f, True)
        deal(k_b, k_f, False)
        quantize_padded(k_x, k_b)
        warm(k_x, R, WARM_B)
        deal(v_b, v_f, True)
        deal(v_b, v_f, False)
        quantize_padded(v_x, v_b)
        warm(v_x, 2 * R * (PACK - 1), WARM_C)
        for h in range(2):
            nc.sync.dma_start(out=v_s[0][:].bitcast(I32)[half(h), :], in_=v_x[0][:].bitcast(I32)[half(1 - h), :])
        nc.sync.dma_start(out=r_f[:], in_=r.rearrange("(c p) n -> p c n", p=P))
        weave(q_b[0], q_f[0], first, True)
        weave(q_b[0], q_f[0], rest, False)
        quantize(q_x[0][1], q_x[0][2], 0, UNIT, q_b[0][:])
        scores(0)
        fill(2, FILL[0])
        weave(q_b[1], q_f[1], first, True)
        weave(q_b[1], q_f[1], rest, False)
        quantize(q_x[1][1], q_x[1][2], 0, UNIT, q_b[1][:])
        scores(1)
        fill(2, FILL[1])
        weigh(0, 0)
        weigh(0, 1)
        weave(wo_b, wo_f, slice(0, R), False)
        quantize_p(0, 0)
        quantize_p(0, 1)
        values(0, 0)
        values(0, 1)
        fill(0, FILL[2])
        weigh(1, 0)
        weigh(1, 1)
        quantize_p(1, 0)
        quantize_p(1, 1)
        values(1, 0)
        values(1, 1)
        quantize(wo_x[1], wo_x[2], 0, O, wo_b[:])
        round_y(0, 0, False)
        round_y(0, 1, False)
        quantize_y(0, 0)
        project(0, 0)
        quantize_y(0, 1)
        project(0, 1)
        round_y(1, 0, False)
        round_y(1, 1, False)
        quantize_y(1, 0)
        finish(0, 0)
        project(1, 0)
        finish(0, 1)
        quantize_y(1, 1)
        project(1, 1)
        finish(1, 0)
        finish(1, 1)
